import numpy as np
import ml_dtypes


def mxq(x, axis, fmt="e4m3"):
    dtype, down = {"e4m3": (ml_dtypes.float8_e4m3fn, 7), "e5m2": (ml_dtypes.float8_e5m2, 14)}[fmt]
    v = np.moveaxis(np.asarray(x, np.float32).astype(ml_dtypes.bfloat16).astype(np.float64), axis, -1)
    blocks = v.reshape(v.shape[:-1] + (-1, 32))
    amax = np.abs(blocks).max(-1, keepdims=True)
    byte = np.maximum(np.where(amax > 0, np.frexp(amax)[1] - 1 + 127, 0) - down, 1)
    scale = np.exp2(byte - 127.0)
    codes = (blocks / scale).astype(np.float32).astype(dtype).astype(np.float64)
    return np.moveaxis((codes * scale).reshape(v.shape), -1, axis)


WIDE = False


def mx_kscale(k):
    if not WIDE:
        return np.ones(k)
    levels = np.array([30, -30])
    if k % 512:
        return np.exp2(np.random.permutation(np.resize(levels, k // 32))).repeat(32)
    a = np.empty((k // 512, 16))
    for p in range(k // 512):
        a[p, :8] = np.random.permutation(np.resize(levels, 8))
        for g in range(8):
            far = levels[np.abs(levels - a[p, g]) >= 10]
            a[p, g + 8] = far[np.random.randint(len(far))]
    return np.exp2(a.ravel()).repeat(32)


def f64(x):
    return np.asarray(x).astype(np.float64)


def striped(idx):
    return np.tile(np.asarray(idx).reshape(-1, 16).T, (8, 1)).astype(np.uint16)


def unstriped(offs):
    return offs[:16].T.reshape(-1).astype(np.int64)


E2M1 = np.array([0.0, 0.5, 1.0, 1.5, 2.0, 3.0, 4.0, 6.0, -0.0, -0.5, -1.0, -1.5, -2.0, -3.0, -4.0, -6.0])


def pack_weight(w, fmt):
    k, n = w.shape
    w = f64(np.asarray(w, np.float32).astype(ml_dtypes.bfloat16)).reshape(k // 32, 32, n)
    amax = np.abs(w).max(1)
    if fmt == "e4m3":
        byte = np.frexp(amax)[1] - 1 + 127 - 7
    else:
        mant, ex = np.frexp(amax / 6.0)
        byte = np.where(mant > 0.5, ex, ex - 1) + 127
    byte = np.clip(np.where(amax > 0, byte, 1), 1, 254)
    scaled = (w * np.exp2(127.0 - byte)[:, None, :]).reshape(k, n).astype(np.float32)
    by_word = np.ascontiguousarray(scaled.reshape(k // 512, 128, 4, n).transpose(0, 1, 3, 2))
    if fmt == "e4m3":
        words = by_word.astype(ml_dtypes.float8_e4m3fn).view(np.uint8)
    else:
        c = by_word.astype(ml_dtypes.float4_e2m1fn).view(np.uint8) & 0xF
        words = (c[..., 0::2] | (c[..., 1::2] << 4)).reshape(k // 512, 128, 2 * n)
    return np.ascontiguousarray(words), np.ascontiguousarray(byte.astype(np.uint8).reshape(k // 512, 16, n))


def unpack_weight(words, scales, fmt):
    g, _, n = scales.shape
    words = np.ascontiguousarray(words).reshape(g, 128, n, -1)
    if fmt == "e4m3":
        vals = words.view(ml_dtypes.float8_e4m3fn).astype(np.float64)
    else:
        nib = np.empty((g, 128, n, 4), np.uint8)
        nib[..., 0::2] = words & 0xF
        nib[..., 1::2] = words >> 4
        vals = E2M1[nib]
    vals = vals * np.repeat(np.exp2(scales.astype(np.float64) - 127.0), 8, axis=1)[..., None]
    return vals.transpose(0, 1, 3, 2).reshape(g * 512, n)


K, T, J, R, O, N, L = 512, 2048, 256, 512, 128, 256, 512


def setup_inputs():
    n = np.random.standard_normal
    idx = np.random.permutation(T)[:J]
    idx2 = np.random.permutation(T)[:J]
    idx3 = np.random.permutation(T)[:J]
    idx4 = np.random.permutation(J)[:O]
    idx5 = np.random.permutation(J)[:O]
    fk = mx_kscale(K)
    fr = mx_kscale(R)
    fl = mx_kscale(L)
    xtp = pack_weight(n((K, T)) / fk[:, None], "e2m1")
    wp = pack_weight(n((K, R)) * 1 / np.sqrt(K) * fk[:, None] * fr, "e4m3")
    wbp = pack_weight(n((R, N)) * 1 / np.sqrt(R) / fr[:, None], "e2m1")
    sxp = pack_weight(n((L, O)) / fl[:, None], "e4m3")
    wsp = pack_weight(n((L, N)) * 1 / np.sqrt(L) * fl[:, None], "e4m3")
    return {
        "xt_words": xtp[0],
        "xt_scales": xtp[1],
        "w_words": wp[0],
        "w_scales": wp[1],
        "wb_words": wbp[0],
        "wb_scales": wbp[1],
        "sx_words": sxp[0],
        "sx_scales": sxp[1],
        "ws_words": wsp[0],
        "ws_scales": wsp[1],
        "offs": striped(idx),
        "offs2": striped(idx2),
        "offs3": striped(idx3),
        "offs4": striped(idx4),
        "offs5": striped(idx5),
    }


def reference(xt_words, xt_scales, w_words, w_scales, wb_words, wb_scales, sx_words, sx_scales, ws_words, ws_scales, offs, offs2, offs3, offs4, offs5):
    idx = unstriped(offs)
    idx2 = unstriped(offs2)
    idx3 = unstriped(offs3)
    idx4 = unstriped(offs4)
    idx5 = unstriped(offs5)
    xtu = unpack_weight(xt_words, xt_scales, "e2m1")
    wu = unpack_weight(w_words, w_scales, "e4m3")
    wbu = unpack_weight(wb_words, wb_scales, "e2m1")
    sxu = unpack_weight(sx_words, sx_scales, "e4m3")
    wsu = unpack_weight(ws_words, ws_scales, "e4m3")
    xtidxg = xtu[:, idx]
    a = wu.T @ xtidxg
    xtidx2g = xtu[:, idx2]
    b = wu.T @ xtidx2g
    xtidx3g = xtu[:, idx3]
    g0 = wu.T @ xtidx3g
    c1 = np.maximum(b, g0)
    hid = np.abs(a[:, idx4] - c1[:, idx5])
    hidq = mxq(hid, 0, "e5m2")
    y = wbu.T @ hidq + wsu.T @ sxu
    return y

@@ -1,0 +1,175 @@
+from contextlib import ExitStack
+
+import concourse.mybir as mybir
+
+K, T, J, R, O, N, L = 512, 2048, 256, 512, 128, 256, 512
+FLOPS = 2 * (3 * K * R * J + R * N * O + L * N * O)
+
+F32 = mybir.dt.float32
+BF16 = mybir.dt.bfloat16
+I32 = mybir.dt.int32
+U32 = mybir.dt.uint32
+U16 = mybir.dt.uint16
+U8 = mybir.dt.uint8
+E4M3X4 = mybir.dt.float8_e4m3fn_x4
+E5M2X4 = mybir.dt.float8_e5m2_x4
+E2M1X4 = mybir.dt.float4_e2m1fn_x4
+ALU = mybir.AluOpType
+ACT = mybir.ActivationFunctionType
+P = 128
+PACK = 4
+
+
+def tile_list_triple_looked_skip_plain_kernel(tc, xt_words, xt_scales, w_words, w_scales, wb_words, wb_scales,
+                                                   sx_words, sx_scales, ws_words, ws_scales,
+                                                   offs, offs2, offs3, offs4, offs5, out):
+    nc = tc.nc
+    with ExitStack() as ctx:
+        lists = ctx.enter_context(tc.tile_pool(name="lists", bufs=1))
+        sb = ctx.enter_context(tc.tile_pool(name="sb", bufs=1))
+        shared = ctx.enter_context(tc.tile_pool(name="shared", bufs=1))
+        psum = ctx.enter_context(tc.psum_pool(name="psum", bufs=1))
+
+        l1 = lists.tile([P, J // 16], U16, name="l1")
+        l2 = lists.tile([P, J // 16], U16, name="l2")
+        l3 = lists.tile([P, J // 16], U16, name="l3")
+        l4 = lists.tile([P, O // 16], U16, name="l4")
+        l5 = lists.tile([P, O // 16], U16, name="l5")
+
+        xw = sb.tile([P, T], U16, name="xw", align_bytes=64)
+        xs = sb.tile([P, T], U8, name="xs", align_bytes=64)
+        ww = sb.tile([P, R], U32, name="ww", align_bytes=64)
+        wsc = shared.tile([P, R], U8, name="wsc", align_bytes=64, offset=256)
+        wbw = sb.tile([P, 2 * N], U8, name="wbw", align_bytes=64)
+        sxw = sb.tile([P, O], U32, name="sxw", align_bytes=64)
+        wsw = sb.tile([P, N], U32, name="wsw", align_bytes=64)
+        late = sb.tile([P, N + O + N], U8, name="late", align_bytes=64)
+        wbs = late[:, 0:N]
+        sxs = late[:, N:N + O]
+        wss = late[:, N + O:N + O + N]
+
+        def rows(eng, plane, src, q):
+            eng.dma_start(out=plane[32 * q:32 * q + 4, :].bitcast(I32), in_=src[0, 4 * q:4 * q + 4, :].bitcast(I32))
+
+        def words(eng, tile, src):
+            eng.dma_start(out=tile[:].bitcast(I32), in_=src.bitcast(I32))
+
+        nc.vector.memset(xs[:].bitcast(I32), 0)
+        nc.gpsimd.memset(wsc[:].bitcast(I32), 0)
+        nc.vector.memset(late[:].bitcast(I32), 0)
+
+        nc.sync.dma_start(l2[:], offs2)
+        nc.sync.dma_start(l1[:], offs)
+        words(nc.sync, xw, xt_words[0])
+        rows(nc.sync, xs, xt_scales, 0)
+        rows(nc.sync, xs, xt_scales, 1)
+        rows(nc.sync, xs, xt_scales, 2)
+        rows(nc.sync, xs, xt_scales, 3)
+        words(nc.sync, ww, w_words[0].rearrange("p n t -> p (n t)"))
+        rows(nc.sync, wsc, w_scales, 0)
+        rows(nc.sync, wsc, w_scales, 1)
+        rows(nc.gpsimd, wsc, w_scales, 2)
+        rows(nc.gpsimd, wsc, w_scales, 3)
+        nc.sync.dma_start(l3[:], offs3)
+        nc.sync.dma_start(l4[:], offs4)
+        nc.sync.dma_start(l5[:], offs5)
+        rows(nc.sync, sxs, sx_scales, 0)
+        rows(nc.sync, sxs, sx_scales, 1)
+        rows(nc.sync, sxs, sx_scales, 2)
+        rows(nc.sync, sxs, sx_scales, 3)
+        rows(nc.sync, wss, ws_scales, 0)
+        rows(nc.sync, wss, ws_scales, 1)
+        rows(nc.sync, wss, ws_scales, 2)
+        rows(nc.sync, wss, ws_scales, 3)
+        words(nc.sync, sxw, sx_words[0].rearrange("p n t -> p (n t)"))
+        words(nc.sync, wsw, ws_words[0].rearrange("p n t -> p (n t)"))
+        words(nc.sync, wbw, wb_words[0])
+        rows(nc.sync, wbs, wb_scales, 0)
+        rows(nc.sync, wbs, wb_scales, 1)
+        rows(nc.sync, wbs, wb_scales, 2)
+        rows(nc.sync, wbs, wb_scales, 3)
+
+        wp = sb.tile([P, R], U32, name="wp", align_bytes=64)
+        wps = sb.tile([P, R], U8, name="wps", align_bytes=64)
+        nc.scalar.copy(out=wp[:].rearrange("p (t q) -> p q t", t=PACK), in_=ww[:].rearrange("p (q t) -> p q t", t=PACK))
+        nc.vector.tensor_copy(out=wps[:].rearrange("p (t q) -> p t q", t=PACK), in_=wsc[:].rearrange("p (q t) -> p t q", t=PACK))
+
+        gw = [None, shared.tile([P, J], U16, name="gw1", align_bytes=64, offset=0), None]
+        gs = [None, shared.tile([P, J], U8, name="gs1", align_bytes=64, offset=512), None]
+        lst = [l2, l1, l3]
+
+        def first(i, t, dst):
+            cols = slice(t * P, (t + 1) * P)
+            nc.tensor.matmul_mx(out=dst, lhsT=wp[:, cols].bitcast(E4M3X4), lhsT_scale=wps[:, cols],
+                                rhs=gw[i][:].bitcast(E2M1X4), rhs_scale=gs[i][:], start=True, stop=True)
+
+        def pick(i):
+            if i != 1:
+                gw[i] = sb.tile([P, J], U16, name="gw%d" % i, tag="gw", align_bytes=64)
+                gs[i] = sb.tile([P, J], U8, name="gs%d" % i, tag="gs", align_bytes=64)
+            nc.vector.tensor_copy(out=gs[i][:], in_=xs[:].indirect(lst[i][:]))
+            nc.vector.tensor_copy(out=gw[i][:], in_=xw[:].indirect(lst[i][:]))
+
+        a_sb = [sb.tile([P, 2 * J], F32, name="a_sb%d" % h) for h in range(2)]
+        b_sb = [sb.tile([P, 2 * J], F32, name="b_sb%d" % h) for h in range(2)]
+        c_sb = [sb.tile([P, J], F32, name="c_sb%d" % t) for t in range(PACK)]
+        ag = sb.tile([P, PACK, O], F32, name="ag")
+        cg = sb.tile([P, PACK, O], F32, name="cg")
+        d = sb.tile([P, PACK, O], F32, name="d")
+
+        pick(0)
+        for h in range(2):
+            bank = psum.tile([P, 2 * J], F32, name="b_ps%d" % h)
+            for u in range(2):
+                first(0, 2 * h + u, bank[:, u * J:(u + 1) * J])
+            nc.scalar.copy(out=b_sb[h][:], in_=bank[:])
+        pick(1)
+        a_ps = []
+        for h in range(2):
+            bank = psum.tile([P, 2 * J], F32, name="a_ps%d" % h)
+            a_ps.append(bank)
+            for u in range(2):
+                first(1, 2 * h + u, bank[:, u * J:(u + 1) * J])
+        nc.scalar.copy(out=a_sb[0][:], in_=a_ps[0][:])
+        pick(2)
+        nc.vector.tensor_copy(out=a_sb[1][:], in_=a_ps[1][:])
+        for t in range(PACK):
+            nc.scalar.activation(out=ag[:, t, :], in_=a_sb[t // 2][:, (t % 2) * J:(t % 2 + 1) * J].indirect(l4[:]), func=ACT.Copy)
+        for t in range(PACK):
+            bank = psum.tile([P, J], F32, name="g_ps%d" % t, tag="g%d" % t)
+            first(2, t, bank[:])
+            nc.vector.tensor_tensor(out=c_sb[t][:], in0=bank[:], in1=b_sb[t // 2][:, (t % 2) * J:(t % 2 + 1) * J], op=ALU.max)
+        accs = []
+        for h in range(2):
+            acc = psum.tile([P, O], F32, name="acc%d" % h, tag="g%d" % h)
+            accs.append(acc)
+            cols = slice(h * P, (h + 1) * P)
+            nc.tensor.matmul_mx(out=acc[:], lhsT=wsw[:, cols].bitcast(E4M3X4), lhsT_scale=wss[:, cols],
+                                rhs=sxw[:].bitcast(E4M3X4), rhs_scale=sxs, start=True, stop=False)
+        KS = 3
+        for t in range(KS):
+            nc.scalar.activation(out=cg[:, t, :], in_=c_sb[t][:].indirect(l5[:]), func=ACT.Copy)
+        for t in range(KS, PACK):
+            nc.vector.tensor_tensor(out=d[:, t, :], in0=c_sb[t][:].indirect(l5[:]), in1=ag[:, t, :], op=ALU.subtract)
+        for (t0, t1) in [(0, 3)]:
+            nc.vector.tensor_tensor(out=d[:, t0:t1, :], in0=cg[:, t0:t1, :], in1=ag[:, t0:t1, :], op=ALU.subtract)
+
+        hb = sb.tile([P, O, PACK], BF16, name="hb", align_bytes=64)
+        SP = 64
+        nc.scalar.activation(out=hb[:, 0:SP, :], in_=d[:, :, 0:SP].rearrange("p t o -> p o t"), func=ACT.Abs)
+        if SP < O:
+            dv = d[:, :, SP:O].rearrange("p t o -> p o t")
+            nc.vector.scalar_tensor_tensor(out=hb[:, SP:O, :], in0=dv, scalar=-1.0, in1=dv, op0=ALU.mult, op1=ALU.max)
+        hq = sb.tile([P, O], U32, name="hq", align_bytes=64)
+        hs = sb.tile([P, O], U8, name="hs", align_bytes=64)
+        nc.vector.quantize_mx(out=hq[:].bitcast(E5M2X4), scales=hs[:], in_=hb[:].rearrange("p o t -> p (o t)"))
+
+        res = [sb.tile([P, O], F32, name="res%d" % h) for h in range(2)]
+        for h in range(2):
+            nc.tensor.matmul_mx(out=accs[h][:], lhsT=wbw[:, 2 * h * P:2 * (h + 1) * P].bitcast(E2M1X4),
+                                lhsT_scale=wbs[:, h * P:(h + 1) * P],
+                                rhs=hq[:].bitcast(E5M2X4), rhs_scale=hs[:], start=False, stop=True)
+        nc.vector.tensor_copy(out=res[0][:], in_=accs[0][:])
+        nc.sync.dma_start(out=out[0:P, :], in_=res[0][:])
+        nc.scalar.copy(out=res[1][:], in_=accs[1][:])
+        nc.scalar.dma_start(out=out[P:2 * P, :], in_=res[1][:])

@@ -39,7 +39,7 @@ def tile_list_triple_looked_skip_plain_kernel(tc, xt_words, xt_scales, w_words, 
         xw = sb.tile([P, T], U16, name="xw", align_bytes=64)
         xs = sb.tile([P, T], U8, name="xs", align_bytes=64)
         ww = sb.tile([P, R], U32, name="ww", align_bytes=64)
-        wsc = shared.tile([P, R], U8, name="wsc", align_bytes=64, offset=256)
+        wsc = shared.tile([P, R], U8, name="wsc", tag="wsc", align_bytes=64)
         wbw = sb.tile([P, 2 * N], U8, name="wbw", align_bytes=64)
         sxw = sb.tile([P, O], U32, name="sxw", align_bytes=64)
         wsw = sb.tile([P, N], U32, name="wsw", align_bytes=64)
@@ -54,22 +54,23 @@ def tile_list_triple_looked_skip_plain_kernel(tc, xt_words, xt_scales, w_words, 
         def words(eng, tile, src):
             eng.dma_start(out=tile[:].bitcast(I32), in_=src.bitcast(I32))
 
-        nc.vector.memset(xs[:].bitcast(I32), 0)
-        nc.gpsimd.memset(wsc[:].bitcast(I32), 0)
+        nc.vector.memset(xs[:, 0:T // 2].bitcast(I32), 0)
+        nc.gpsimd.memset(xs[:, T // 2:T].bitcast(I32), 0)
+        nc.vector.memset(wsc[:].bitcast(I32), 0)
         nc.vector.memset(late[:].bitcast(I32), 0)
 
         nc.sync.dma_start(l2[:], offs2)
+        words(nc.scalar, ww, w_words[0].rearrange("p n t -> p (n t)"))
         nc.sync.dma_start(l1[:], offs)
-        words(nc.sync, xw, xt_words[0])
         rows(nc.sync, xs, xt_scales, 0)
         rows(nc.sync, xs, xt_scales, 1)
         rows(nc.sync, xs, xt_scales, 2)
         rows(nc.sync, xs, xt_scales, 3)
-        words(nc.sync, ww, w_words[0].rearrange("p n t -> p (n t)"))
+        words(nc.sync, xw, xt_words[0])
         rows(nc.sync, wsc, w_scales, 0)
         rows(nc.sync, wsc, w_scales, 1)
-        rows(nc.gpsimd, wsc, w_scales, 2)
-        rows(nc.gpsimd, wsc, w_scales, 3)
+        rows(nc.sync, wsc, w_scales, 2)
+        rows(nc.sync, wsc, w_scales, 3)
         nc.sync.dma_start(l3[:], offs3)
         nc.sync.dma_start(l4[:], offs4)
         nc.sync.dma_start(l5[:], offs5)
@@ -94,8 +95,8 @@ def tile_list_triple_looked_skip_plain_kernel(tc, xt_words, xt_scales, w_words, 
         nc.scalar.copy(out=wp[:].rearrange("p (t q) -> p q t", t=PACK), in_=ww[:].rearrange("p (q t) -> p q t", t=PACK))
         nc.vector.tensor_copy(out=wps[:].rearrange("p (t q) -> p t q", t=PACK), in_=wsc[:].rearrange("p (q t) -> p t q", t=PACK))
 
-        gw = [None, shared.tile([P, J], U16, name="gw1", align_bytes=64, offset=0), None]
-        gs = [None, shared.tile([P, J], U8, name="gs1", align_bytes=64, offset=512), None]
+        gw = [sb.tile([P, J], U16, name="gw0", align_bytes=64), shared.tile([P, J], U16, name="gw1", tag="wsc", align_bytes=64), sb.tile([P, J], U16, name="gw2", align_bytes=64)]
+        gs = [sb.tile([P, J], U8, name="gs%d" % i, align_bytes=64) for i in range(3)]
         lst = [l2, l1, l3]
 
         def first(i, t, dst):
@@ -104,9 +105,6 @@ def tile_list_triple_looked_skip_plain_kernel(tc, xt_words, xt_scales, w_words, 
                                 rhs=gw[i][:].bitcast(E2M1X4), rhs_scale=gs[i][:], start=True, stop=True)
 
         def pick(i):
-            if i != 1:
-                gw[i] = sb.tile([P, J], U16, name="gw%d" % i, tag="gw", align_bytes=64)
-                gs[i] = sb.tile([P, J], U8, name="gs%d" % i, tag="gs", align_bytes=64)
             nc.vector.tensor_copy(out=gs[i][:], in_=xs[:].indirect(lst[i][:]))
             nc.vector.tensor_copy(out=gw[i][:], in_=xw[:].indirect(lst[i][:]))
 
@@ -130,9 +128,9 @@ def tile_list_triple_looked_skip_plain_kernel(tc, xt_words, xt_scales, w_words, 
             a_ps.append(bank)
             for u in range(2):
                 first(1, 2 * h + u, bank[:, u * J:(u + 1) * J])
-        nc.scalar.copy(out=a_sb[0][:], in_=a_ps[0][:])
         pick(2)
-        nc.vector.tensor_copy(out=a_sb[1][:], in_=a_ps[1][:])
+        nc.vector.tensor_copy(out=a_sb[0][:], in_=a_ps[0][:])
+        nc.scalar.copy(out=a_sb[1][:], in_=a_ps[1][:])
         for t in range(PACK):
             nc.scalar.activation(out=ag[:, t, :], in_=a_sb[t // 2][:, (t % 2) * J:(t % 2 + 1) * J].indirect(l4[:]), func=ACT.Copy)
         for t in range(PACK):
@@ -141,17 +139,17 @@ def tile_list_triple_looked_skip_plain_kernel(tc, xt_words, xt_scales, w_words, 
             nc.vector.tensor_tensor(out=c_sb[t][:], in0=bank[:], in1=b_sb[t // 2][:, (t % 2) * J:(t % 2 + 1) * J], op=ALU.max)
         accs = []
         for h in range(2):
-            acc = psum.tile([P, O], F32, name="acc%d" % h, tag="g%d" % h)
+            acc = psum.tile([P, O], F32, name="acc%d" % h, tag="g%d" % (2 + h))
             accs.append(acc)
             cols = slice(h * P, (h + 1) * P)
             nc.tensor.matmul_mx(out=acc[:], lhsT=wsw[:, cols].bitcast(E4M3X4), lhsT_scale=wss[:, cols],
                                 rhs=sxw[:].bitcast(E4M3X4), rhs_scale=sxs, start=True, stop=False)
-        KS = 3
+        KS = 0
         for t in range(KS):
             nc.scalar.activation(out=cg[:, t, :], in_=c_sb[t][:].indirect(l5[:]), func=ACT.Copy)
         for t in range(KS, PACK):
             nc.vector.tensor_tensor(out=d[:, t, :], in0=c_sb[t][:].indirect(l5[:]), in1=ag[:, t, :], op=ALU.subtract)
-        for (t0, t1) in [(0, 3)]:
+        for (t0, t1) in []:
             nc.vector.tensor_tensor(out=d[:, t0:t1, :], in0=cg[:, t0:t1, :], in1=ag[:, t0:t1, :], op=ALU.subtract)
 
         hb = sb.tile([P, O, PACK], BF16, name="hb", align_bytes=64)

from contextlib import ExitStack

import concourse.mybir as mybir

K, T, J, R, O, N, L = 512, 2048, 256, 512, 128, 256, 512
FLOPS = 2 * (3 * K * R * J + R * N * O + L * N * O)

F32 = mybir.dt.float32
BF16 = mybir.dt.bfloat16
I32 = mybir.dt.int32
U32 = mybir.dt.uint32
U16 = mybir.dt.uint16
U8 = mybir.dt.uint8
E4M3X4 = mybir.dt.float8_e4m3fn_x4
E5M2X4 = mybir.dt.float8_e5m2_x4
E2M1X4 = mybir.dt.float4_e2m1fn_x4
ALU = mybir.AluOpType
ACT = mybir.ActivationFunctionType
P = 128
PACK = 4


def tile_list_triple_looked_skip_plain_kernel(tc, xt_words, xt_scales, w_words, w_scales, wb_words, wb_scales,
                                                   sx_words, sx_scales, ws_words, ws_scales,
                                                   offs, offs2, offs3, offs4, offs5, out):
    nc = tc.nc
    with ExitStack() as ctx:
        lists = ctx.enter_context(tc.tile_pool(name="lists", bufs=1))
        sb = ctx.enter_context(tc.tile_pool(name="sb", bufs=1))
        shared = ctx.enter_context(tc.tile_pool(name="shared", bufs=1))
        psum = ctx.enter_context(tc.psum_pool(name="psum", bufs=1))

        l1 = lists.tile([P, J // 16], U16, name="l1")
        l2 = lists.tile([P, J // 16], U16, name="l2")
        l3 = lists.tile([P, J // 16], U16, name="l3")
        l4 = lists.tile([P, O // 16], U16, name="l4")
        l5 = lists.tile([P, O // 16], U16, name="l5")

        xw = sb.tile([P, T], U16, name="xw", align_bytes=64)
        xs = sb.tile([P, T], U8, name="xs", align_bytes=64)
        ww = sb.tile([P, R], U32, name="ww", align_bytes=64)
        wsc = shared.tile([P, R], U8, name="wsc", tag="wsc", align_bytes=64)
        wbw = sb.tile([P, 2 * N], U8, name="wbw", align_bytes=64)
        sxw = sb.tile([P, O], U32, name="sxw", align_bytes=64)
        wsw = sb.tile([P, N], U32, name="wsw", align_bytes=64)
        late = sb.tile([P, N + O + N], U8, name="late", align_bytes=64)
        wbs = late[:, 0:N]
        sxs = late[:, N:N + O]
        wss = late[:, N + O:N + O + N]

        def rows(eng, plane, src, q):
            eng.dma_start(out=plane[32 * q:32 * q + 4, :].bitcast(I32), in_=src[0, 4 * q:4 * q + 4, :].bitcast(I32))

        def words(eng, tile, src):
            eng.dma_start(out=tile[:].bitcast(I32), in_=src.bitcast(I32))

        nc.vector.memset(xs[:, 0:T // 2].bitcast(I32), 0)
        nc.gpsimd.memset(xs[:, T // 2:T].bitcast(I32), 0)
        nc.vector.memset(wsc[:].bitcast(I32), 0)
        nc.vector.memset(late[:].bitcast(I32), 0)

        nc.sync.dma_start(l2[:], offs2)
        words(nc.scalar, ww, w_words[0].rearrange("p n t -> p (n t)"))
        nc.sync.dma_start(l1[:], offs)
        rows(nc.sync, xs, xt_scales, 0)
        rows(nc.sync, xs, xt_scales, 1)
        rows(nc.sync, xs, xt_scales, 2)
        rows(nc.sync, xs, xt_scales, 3)
        words(nc.sync, xw, xt_words[0])
        rows(nc.sync, wsc, w_scales, 0)
        rows(nc.sync, wsc, w_scales, 1)
        rows(nc.sync, wsc, w_scales, 2)
        rows(nc.sync, wsc, w_scales, 3)
        nc.sync.dma_start(l3[:], offs3)
        nc.sync.dma_start(l4[:], offs4)
        nc.sync.dma_start(l5[:], offs5)
        rows(nc.sync, sxs, sx_scales, 0)
        rows(nc.sync, sxs, sx_scales, 1)
        rows(nc.sync, sxs, sx_scales, 2)
        rows(nc.sync, sxs, sx_scales, 3)
        rows(nc.sync, wss, ws_scales, 0)
        rows(nc.sync, wss, ws_scales, 1)
        rows(nc.sync, wss, ws_scales, 2)
        rows(nc.sync, wss, ws_scales, 3)
        words(nc.sync, sxw, sx_words[0].rearrange("p n t -> p (n t)"))
        words(nc.sync, wsw, ws_words[0].rearrange("p n t -> p (n t)"))
        words(nc.sync, wbw, wb_words[0])
        rows(nc.sync, wbs, wb_scales, 0)
        rows(nc.sync, wbs, wb_scales, 1)
        rows(nc.sync, wbs, wb_scales, 2)
        rows(nc.sync, wbs, wb_scales, 3)

        wp = sb.tile([P, R], U32, name="wp", align_bytes=64)
        wps = sb.tile([P, R], U8, name="wps", align_bytes=64)
        nc.scalar.copy(out=wp[:].rearrange("p (t q) -> p q t", t=PACK), in_=ww[:].rearrange("p (q t) -> p q t", t=PACK))
        nc.vector.tensor_copy(out=wps[:].rearrange("p (t q) -> p t q", t=PACK), in_=wsc[:].rearrange("p (q t) -> p t q", t=PACK))

        gw = [sb.tile([P, J], U16, name="gw0", align_bytes=64), shared.tile([P, J], U16, name="gw1", tag="wsc", align_bytes=64), sb.tile([P, J], U16, name="gw2", align_bytes=64)]
        gs = [sb.tile([P, J], U8, name="gs%d" % i, align_bytes=64) for i in range(3)]
        lst = [l2, l1, l3]

        def first(i, t, dst):
            cols = slice(t * P, (t + 1) * P)
            nc.tensor.matmul_mx(out=dst, lhsT=wp[:, cols].bitcast(E4M3X4), lhsT_scale=wps[:, cols],
                                rhs=gw[i][:].bitcast(E2M1X4), rhs_scale=gs[i][:], start=True, stop=True)

        def pick(i):
            nc.vector.tensor_copy(out=gs[i][:], in_=xs[:].indirect(lst[i][:]))
            nc.vector.tensor_copy(out=gw[i][:], in_=xw[:].indirect(lst[i][:]))

        a_sb = [sb.tile([P, 2 * J], F32, name="a_sb%d" % h) for h in range(2)]
        b_sb = [sb.tile([P, 2 * J], F32, name="b_sb%d" % h) for h in range(2)]
        c_sb = [sb.tile([P, J], F32, name="c_sb%d" % t) for t in range(PACK)]
        ag = sb.tile([P, PACK, O], F32, name="ag")
        cg = sb.tile([P, PACK, O], F32, name="cg")
        d = sb.tile([P, PACK, O], F32, name="d")

        pick(0)
        for h in range(2):
            bank = psum.tile([P, 2 * J], F32, name="b_ps%d" % h)
            for u in range(2):
                first(0, 2 * h + u, bank[:, u * J:(u + 1) * J])
            nc.scalar.copy(out=b_sb[h][:], in_=bank[:])
        pick(1)
        a_ps = []
        for h in range(2):
            bank = psum.tile([P, 2 * J], F32, name="a_ps%d" % h)
            a_ps.append(bank)
            for u in range(2):
                first(1, 2 * h + u, bank[:, u * J:(u + 1) * J])
        pick(2)
        nc.vector.tensor_copy(out=a_sb[0][:], in_=a_ps[0][:])
        nc.scalar.copy(out=a_sb[1][:], in_=a_ps[1][:])
        for t in range(PACK):
            nc.scalar.activation(out=ag[:, t, :], in_=a_sb[t // 2][:, (t % 2) * J:(t % 2 + 1) * J].indirect(l4[:]), func=ACT.Copy)
        for t in range(PACK):
            bank = psum.tile([P, J], F32, name="g_ps%d" % t, tag="g%d" % t)
            first(2, t, bank[:])
            nc.vector.tensor_tensor(out=c_sb[t][:], in0=bank[:], in1=b_sb[t // 2][:, (t % 2) * J:(t % 2 + 1) * J], op=ALU.max)
        accs = []
        for h in range(2):
            acc = psum.tile([P, O], F32, name="acc%d" % h, tag="g%d" % (2 + h))
            accs.append(acc)
            cols = slice(h * P, (h + 1) * P)
            nc.tensor.matmul_mx(out=acc[:], lhsT=wsw[:, cols].bitcast(E4M3X4), lhsT_scale=wss[:, cols],
                                rhs=sxw[:].bitcast(E4M3X4), rhs_scale=sxs, start=True, stop=False)
        KS = 0
        for t in range(KS):
            nc.scalar.activation(out=cg[:, t, :], in_=c_sb[t][:].indirect(l5[:]), func=ACT.Copy)
        for t in range(KS, PACK):
            nc.vector.tensor_tensor(out=d[:, t, :], in0=c_sb[t][:].indirect(l5[:]), in1=ag[:, t, :], op=ALU.subtract)
        for (t0, t1) in []:
            nc.vector.tensor_tensor(out=d[:, t0:t1, :], in0=cg[:, t0:t1, :], in1=ag[:, t0:t1, :], op=ALU.subtract)

        hb = sb.tile([P, O, PACK], BF16, name="hb", align_bytes=64)
        SP = 64
        nc.scalar.activation(out=hb[:, 0:SP, :], in_=d[:, :, 0:SP].rearrange("p t o -> p o t"), func=ACT.Abs)
        if SP < O:
            dv = d[:, :, SP:O].rearrange("p t o -> p o t")
            nc.vector.scalar_tensor_tensor(out=hb[:, SP:O, :], in0=dv, scalar=-1.0, in1=dv, op0=ALU.mult, op1=ALU.max)
        hq = sb.tile([P, O], U32, name="hq", align_bytes=64)
        hs = sb.tile([P, O], U8, name="hs", align_bytes=64)
        nc.vector.quantize_mx(out=hq[:].bitcast(E5M2X4), scales=hs[:], in_=hb[:].rearrange("p o t -> p (o t)"))

        res = [sb.tile([P, O], F32, name="res%d" % h) for h in range(2)]
        for h in range(2):
            nc.tensor.matmul_mx(out=accs[h][:], lhsT=wbw[:, 2 * h * P:2 * (h + 1) * P].bitcast(E2M1X4),
                                lhsT_scale=wbs[:, h * P:(h + 1) * P],
                                rhs=hq[:].bitcast(E5M2X4), rhs_scale=hs[:], start=False, stop=True)
        nc.vector.tensor_copy(out=res[0][:], in_=accs[0][:])
        nc.sync.dma_start(out=out[0:P, :], in_=res[0][:])
        nc.scalar.copy(out=res[1][:], in_=accs[1][:])
        nc.scalar.dma_start(out=out[P:2 * P, :], in_=res[1][:])
